import numpy as np
import ml_dtypes


def mxq(x, axis, fmt="e4m3"):
    dtype, down = {"e4m3": (ml_dtypes.float8_e4m3fn, 7), "e5m2": (ml_dtypes.float8_e5m2, 14)}[fmt]
    v = np.moveaxis(np.asarray(x, np.float32).astype(ml_dtypes.bfloat16).astype(np.float64), axis, -1)
    blocks = v.reshape(v.shape[:-1] + (-1, 32))
    amax = np.abs(blocks).max(-1, keepdims=True)
    byte = np.maximum(np.where(amax > 0, np.frexp(amax)[1] - 1 + 127, 0) - down, 1)
    scale = np.exp2(byte - 127.0)
    codes = (blocks / scale).astype(np.float32).astype(dtype).astype(np.float64)
    return np.moveaxis((codes * scale).reshape(v.shape), -1, axis)


WIDE = False


def mx_kscale(k):
    if not WIDE:
        return np.ones(k)
    levels = np.array([10, -10, 5, -5, 0])
    if k % 512:
        return np.exp2(np.random.permutation(np.resize(levels, k // 32))).repeat(32)
    a = np.empty((k // 512, 16))
    for p in range(k // 512):
        a[p, :8] = np.random.permutation(np.resize(levels, 8))
        for g in range(8):
            far = levels[np.abs(levels - a[p, g]) >= 10]
            a[p, g + 8] = far[np.random.randint(len(far))]
    return np.exp2(a.ravel()).repeat(32)


def f64(x):
    return np.asarray(x).astype(np.float64)


def striped(idx):
    return np.tile(idx.reshape(-1, 16).T, (8, 1)).astype(np.uint16)


def unstriped(offs):
    return offs[:16].T.reshape(-1).astype(np.int64)


def pack_weight(w):
    k, n = w.shape
    w = f64(np.asarray(w, np.float32).astype(ml_dtypes.bfloat16)).reshape(k // 32, 32, n)
    amax = np.abs(w).max(1)
    byte = np.clip(np.where(amax > 0, np.frexp(amax)[1] - 1 + 127 - 7, 1), 1, 254)
    scaled = (w * np.exp2(127.0 - byte)[:, None, :]).reshape(k, n).astype(np.float32)
    words = np.ascontiguousarray(scaled.reshape(k // 512, 128, 4, n).transpose(0, 1, 3, 2)).astype(ml_dtypes.float8_e4m3fn).view(np.uint8)
    return words, np.ascontiguousarray(byte.astype(np.uint8).reshape(k // 512, 16, n))


def unpack_weight(words, scales):
    g, p, n, _ = words.shape
    vals = np.ascontiguousarray(words).view(ml_dtypes.float8_e4m3fn).astype(np.float64) * np.repeat(np.exp2(scales.astype(np.float64) - 127.0), 8, axis=1)[..., None]
    return vals.transpose(0, 1, 3, 2).reshape(g * 512, n)


K, T, S, N, U = 512, 1024, 512, 128, 512
P = 2 ** 7


def setup_inputs():
    n = np.random.standard_normal
    s = mx_kscale(K)[:, None]
    packed_xT = pack_weight(n((K, T)) * s)
    return {
        "x_words": packed_xT[0],
        "x_scales": packed_xT[1],
        "w1": (n((K, N)) / np.sqrt(K) / s).astype(np.float32),
        "w2": (n((K, N)) / np.sqrt(K) / s).astype(np.float32),
        "inp": (np.tile(np.random.uniform(0.1, 1.0, U), (P, 1))).astype(np.float32),
        "fee": (np.tile(np.random.uniform(0.9, 0.999, U), (P, 1))).astype(np.float32),
        "risk": (np.random.uniform(0.1, 0.6, (N, 1))).astype(np.float32),
        "offs": striped(np.random.permutation(T)[:S]),
        "hop1": striped(np.random.randint(0, S, U)),
        "hop2": striped(np.random.randint(0, S, U)),
    }


def reference(x_words, x_scales, w1, w2, inp, fee, risk, offs, hop1, hop2):
    xq = unpack_weight(x_words, x_scales)[:, unstriped(offs)]
    yb = mxq(f64(w2), 0, "e4m3").T @ xq
    rb = np.log(np.exp(yb) + 1.0) + 0.5
    ya = mxq(f64(w1), 0, "e4m3").T @ xq
    ra = np.log(np.exp(ya) + 1.0) + 0.5
    mid = (rb[:, unstriped(hop1)] * (f64(inp)[:1] * f64(fee)[:1])) / (ra[:, unstriped(hop1)] + f64(inp)[:1] * f64(fee)[:1])
    got = (rb[:, unstriped(hop2)] * (mid * f64(fee)[:1])) / (ra[:, unstriped(hop2)] + mid * f64(fee)[:1])
    return got - (f64(risk) * ((mid) ** 2))

@@ -1,0 +1,184 @@
+import math
+from contextlib import ExitStack
+
+import concourse.mybir as mybir
+
+K, T, S, N, U = 512, 1024, 512, 128, 512
+FLOPS = 2 * 2 * K * N * S
+
+F32 = mybir.dt.float32
+BF16 = mybir.dt.bfloat16
+I32 = mybir.dt.int32
+U32 = mybir.dt.uint32
+U16 = mybir.dt.uint16
+U8 = mybir.dt.uint8
+FP8X4 = mybir.dt.float8_e4m3fn_x4
+ALU = mybir.AluOpType
+ACT = mybir.ActivationFunctionType
+
+P = 128
+PACK = 4
+LIST_ROWS = 16
+POOL_PARTS = [(0, 256), (256, 512)]
+ROUTE_PARTS = [(0, 256), (256, 512)]
+LN_FACTOR = 0.5 * math.exp(-0.5)
+
+
+def tile_picked_yamm_net_p_kernel(
+    tc, x_words, x_scales, w1, w2, inp, fee, risk, offs, hop1, hop2, out
+):
+    nc = tc.nc
+    with ExitStack() as ctx:
+        keep = ctx.enter_context(tc.tile_pool(name="keep", bufs=1))
+        psum = ctx.enter_context(tc.psum_pool(name="psum", bufs=1))
+
+        def f32_tile(name, width):
+            return keep.tile([P, width], F32, name=name, align_bytes=64)
+
+        def entries(list_tile, lo, hi):
+            return list_tile[:, lo // LIST_ROWS : hi // LIST_ROWS]
+
+        offs_sb = keep.tile([P, S // LIST_ROWS], U16, name="offs_sb")
+        hop1_sb = keep.tile([P, U // LIST_ROWS], U16, name="hop1_sb")
+        hop2_sb = keep.tile([P, U // LIST_ROWS], U16, name="hop2_sb")
+        table_words = keep.tile([P, T], U32, name="table_words", align_bytes=64)
+        table_scales = keep.tile([P, T], U8, name="table_scales", align_bytes=64)
+        w_raw = [keep.tile([P, PACK, N], F32, name="w_raw%d" % i, align_bytes=64) for i in range(2)]
+        inp_sb = f32_tile("inp_sb", U)
+        fee_sb = f32_tile("fee_sb", U)
+        risk_sb = f32_tile("risk_sb", 1)
+        preload = f32_tile("preload", 1)
+        preload_out = f32_tile("preload_out", 3)
+
+        nc.vector.memset(table_scales[:].bitcast(I32), 0)
+        nc.vector.memset(preload[:], 1.0)
+        ln_bias = f32_tile("ln_bias", 1)
+        nc.vector.tensor_scalar_mul(ln_bias[:], preload[:], LN_FACTOR)
+        nc.scalar.activation(preload_out[:, 0:1], preload[:], ACT.Tanh)
+
+        nc.sync.dma_start(offs_sb[:], offs)
+        nc.sync.dma_start(w_raw[0][:], w1.rearrange("(p j) n -> p j n", j=PACK))
+        nc.sync.dma_start(w_raw[1][:], w2.rearrange("(p j) n -> p j n", j=PACK))
+        scale_rows = x_scales[0].bitcast(I32)
+        for q in range(4):
+            nc.sync.dma_start(table_scales[32 * q : 32 * q + 4, :].bitcast(I32), scale_rows[4 * q : 4 * q + 4, :])
+        nc.sync.dma_start(table_words[:].bitcast(I32), x_words[0].rearrange("p c r -> p (c r)").bitcast(I32))
+        nc.sync.dma_start(hop1_sb[:], hop1)
+        nc.sync.dma_start(inp_sb[:], inp)
+        nc.sync.dma_start(fee_sb[:], fee)
+        nc.sync.dma_start(hop2_sb[:], hop2)
+        nc.sync.dma_start(risk_sb[:], risk)
+
+        picked_scales = keep.tile([P, S], U8, name="picked_scales", align_bytes=64)
+        picked_words = keep.tile([P, S], U32, name="picked_words", align_bytes=64)
+        w_codes = [keep.tile([P, N], U32, name="w_codes%d" % i, align_bytes=64) for i in range(2)]
+        w_scales = [keep.tile([P, N], U8, name="w_scales%d" % i, align_bytes=64) for i in range(2)]
+        w_grouped = [keep.tile([P, N, PACK], BF16, name="w_grouped%d" % i, align_bytes=64) for i in range(2)]
+
+        def quantize_weight(i):
+            nc.scalar.copy(w_grouped[i][:], w_raw[i][:].rearrange("p j n -> p n j"))
+            nc.vector.quantize_mx(
+                out=w_codes[i][:].bitcast(FP8X4),
+                scales=w_scales[i][:],
+                in_=w_grouped[i][:].rearrange("p n j -> p (n j)"),
+            )
+
+        quantize_weight(0)
+        quantize_weight(1)
+        nc.vector.tensor_copy(picked_scales[:], table_scales[:].indirect(offs_sb[:]))
+        for lo, hi in POOL_PARTS:
+            nc.vector.tensor_copy(picked_words[:, lo:hi], table_words[:].indirect(entries(offs_sb, lo, hi)))
+
+        y = [[psum.tile([P, hi - lo], F32, name="y%d_%d" % (i, lo)) for lo, hi in POOL_PARTS] for i in range(2)]
+        tanh_half = [f32_tile("tanh_half%d" % i, S) for i in range(2)]
+        abs_tanh = [f32_tile("abs_tanh%d" % i, S) for i in range(2)]
+        log_term = [f32_tile("log_term%d" % i, S) for i in range(2)]
+        reserve = [f32_tile("reserve%d" % i, S) for i in range(2)]
+        for h, (lo, hi) in enumerate(POOL_PARTS):
+            for i in range(2):
+                nc.tensor.matmul_mx(
+                    out=y[i][h][:],
+                    lhsT=w_codes[i][:].bitcast(FP8X4),
+                    lhsT_scale=w_scales[i][:],
+                    rhs=picked_words[:, lo:hi].bitcast(FP8X4),
+                    rhs_scale=picked_scales[:, lo:hi],
+                    start=True,
+                    stop=True,
+                )
+                nc.scalar.activation(tanh_half[i][:, lo:hi], y[i][h][:], ACT.Tanh, scale=0.5)
+        nc.scalar.activation(preload_out[:, 1:2], tanh_half[1][:, S - 1 : S], ACT.Ln, scale=0.0, bias=ln_bias[:])
+
+        paid = f32_tile("paid", U)
+        neg_risk = f32_tile("neg_risk", 1)
+        for i in range(2):
+            nc.vector.scalar_tensor_tensor(abs_tanh[i][:], tanh_half[i][:], -1.0, tanh_half[i][:], ALU.mult, ALU.max)
+        nc.vector.tensor_tensor(paid[:], inp_sb[:], fee_sb[:], ALU.mult)
+        nc.vector.tensor_scalar_mul(neg_risk[:], risk_sb[:], -1.0)
+
+        for i in range(2):
+            for h, (lo, hi) in enumerate(POOL_PARTS):
+                nc.scalar.activation(log_term[i][:, lo:hi], abs_tanh[i][:, lo:hi], ACT.Ln, scale=LN_FACTOR, bias=ln_bias[:])
+        nc.scalar.activation(preload_out[:, 2:3], log_term[1][:, S - 1 : S], ACT.Abs_reciprocal_sqrt, scale=0.0, bias=ln_bias[:])
+
+        def finish_reserve(i):
+            for h, (lo, hi) in enumerate(POOL_PARTS):
+                nc.vector.scalar_tensor_tensor(
+                    reserve[i][:, lo:hi], y[i][h][:], 0.0, log_term[i][:, lo:hi], ALU.max, ALU.subtract
+                )
+
+        ra, rb = reserve
+        names = ["den", "num", "sign", "root", "recip", "signed", "quot"]
+        hop = [{n: [f32_tile("%s%d_%d" % (n, k, lo), hi - lo) for lo, hi in ROUTE_PARTS] for n in names} for k in range(2)]
+        passed = [f32_tile("passed%d" % lo, hi - lo) for lo, hi in ROUTE_PARTS]
+        mid_sq = [f32_tile("mid_sq%d" % lo, hi - lo) for lo, hi in ROUTE_PARTS]
+        result = [f32_tile("result%d" % lo, hi - lo) for lo, hi in ROUTE_PARTS]
+
+        def denominator(k, c, list_tile, amount):
+            lo, hi = ROUTE_PARTS[c]
+            t = hop[k]
+            nc.vector.tensor_tensor(t["den"][c][:], ra[:].indirect(entries(list_tile, lo, hi)), amount, ALU.add)
+            nc.scalar.activation(t["sign"][c][:], t["den"][c][:], ACT.Sign)
+            nc.scalar.activation(t["root"][c][:], t["den"][c][:], ACT.Abs_reciprocal_sqrt)
+            nc.scalar.activation(t["recip"][c][:], t["root"][c][:], ACT.Square)
+
+        def numerator(k, c, list_tile, amount):
+            lo, hi = ROUTE_PARTS[c]
+            nc.vector.tensor_tensor(hop[k]["num"][c][:], rb[:].indirect(entries(list_tile, lo, hi)), amount, ALU.mult)
+
+        def signed(k, c):
+            t = hop[k]
+            nc.vector.tensor_tensor(t["signed"][c][:], t["num"][c][:], t["sign"][c][:], ALU.mult)
+
+        def quotient(k, c):
+            t = hop[k]
+            nc.vector.tensor_tensor(t["quot"][c][:], t["signed"][c][:], t["recip"][c][:], ALU.mult)
+
+        parts = range(len(ROUTE_PARTS))
+        finish_reserve(0)
+        for c in parts:
+            denominator(0, c, hop1_sb, paid[:, ROUTE_PARTS[c][0] : ROUTE_PARTS[c][1]])
+        finish_reserve(1)
+        for c in parts:
+            numerator(0, c, hop1_sb, paid[:, ROUTE_PARTS[c][0] : ROUTE_PARTS[c][1]])
+        for c in parts:
+            signed(0, c)
+        for c in parts:
+            quotient(0, c)
+        for c in parts:
+            lo, hi = ROUTE_PARTS[c]
+            nc.vector.tensor_tensor(passed[c][:], hop[0]["quot"][c][:], fee_sb[:, lo:hi], ALU.mult)
+        for c in parts:
+            denominator(1, c, hop2_sb, passed[c][:])
+        for c in parts:
+            nc.scalar.activation(mid_sq[c][:], hop[0]["quot"][c][:], ACT.Square)
+            numerator(1, c, hop2_sb, passed[c][:])
+        for c in parts:
+            signed(1, c)
+        for c in parts:
+            quotient(1, c)
+        for c in parts:
+            lo, hi = ROUTE_PARTS[c]
+            nc.vector.scalar_tensor_tensor(
+                result[c][:], mid_sq[c][:], neg_risk[:], hop[1]["quot"][c][:], ALU.mult, ALU.add
+            )
+            nc.sync.dma_start(out[:, lo:hi], result[c][:])

@@ -19,7 +19,8 @@ ACT = mybir.ActivationFunctionType
 P = 128
 PACK = 4
 LIST_ROWS = 16
-POOL_PARTS = [(0, 256), (256, 512)]
+POOL_PARTS = [(0, 128), (128, 256), (256, 384), (384, 512)]
+LOG_PARTS = [(0, 256), (256, 512)]
 ROUTE_PARTS = [(0, 256), (256, 512)]
 LN_FACTOR = 0.5 * math.exp(-0.5)
 
@@ -56,12 +57,12 @@ def tile_picked_yamm_net_p_kernel(
         nc.vector.tensor_scalar_mul(ln_bias[:], preload[:], LN_FACTOR)
         nc.scalar.activation(preload_out[:, 0:1], preload[:], ACT.Tanh)
 
-        nc.sync.dma_start(offs_sb[:], offs)
         nc.sync.dma_start(w_raw[0][:], w1.rearrange("(p j) n -> p j n", j=PACK))
-        nc.sync.dma_start(w_raw[1][:], w2.rearrange("(p j) n -> p j n", j=PACK))
+        nc.sync.dma_start(offs_sb[:], offs)
         scale_rows = x_scales[0].bitcast(I32)
         for q in range(4):
             nc.sync.dma_start(table_scales[32 * q : 32 * q + 4, :].bitcast(I32), scale_rows[4 * q : 4 * q + 4, :])
+        nc.sync.dma_start(w_raw[1][:], w2.rearrange("(p j) n -> p j n", j=PACK))
         nc.sync.dma_start(table_words[:].bitcast(I32), x_words[0].rearrange("p c r -> p (c r)").bitcast(I32))
         nc.sync.dma_start(hop1_sb[:], hop1)
         nc.sync.dma_start(inp_sb[:], inp)
@@ -70,115 +71,105 @@ def tile_picked_yamm_net_p_kernel(
         nc.sync.dma_start(risk_sb[:], risk)
 
         picked_scales = keep.tile([P, S], U8, name="picked_scales", align_bytes=64)
-        picked_words = keep.tile([P, S], U32, name="picked_words", align_bytes=64)
-        w_codes = [keep.tile([P, N], U32, name="w_codes%d" % i, align_bytes=64) for i in range(2)]
-        w_scales = [keep.tile([P, N], U8, name="w_scales%d" % i, align_bytes=64) for i in range(2)]
-        w_grouped = [keep.tile([P, N, PACK], BF16, name="w_grouped%d" % i, align_bytes=64) for i in range(2)]
+        picked_words = [
+            keep.tile([P, hi - lo], U32, name="picked_words%d" % lo, align_bytes=64) for lo, hi in POOL_PARTS
+        ]
+        w_codes = keep.tile([P, 2 * N], U32, name="w_codes", align_bytes=64)
+        w_scales = keep.tile([P, 2 * N], U8, name="w_scales", align_bytes=64)
+        w_grouped = keep.tile([P, 2 * N * PACK], BF16, name="w_grouped", align_bytes=64)
 
-        def quantize_weight(i):
-            nc.scalar.copy(w_grouped[i][:], w_raw[i][:].rearrange("p j n -> p n j"))
-            nc.vector.quantize_mx(
-                out=w_codes[i][:].bitcast(FP8X4),
-                scales=w_scales[i][:],
-                in_=w_grouped[i][:].rearrange("p n j -> p (n j)"),
-            )
-
-        quantize_weight(0)
-        quantize_weight(1)
         nc.vector.tensor_copy(picked_scales[:], table_scales[:].indirect(offs_sb[:]))
-        for lo, hi in POOL_PARTS:
-            nc.vector.tensor_copy(picked_words[:, lo:hi], table_words[:].indirect(entries(offs_sb, lo, hi)))
+        for i in range(2):
+            nc.scalar.copy(
+                w_grouped[:, i * N * PACK : (i + 1) * N * PACK].rearrange("p (n j) -> p n j", j=PACK),
+                w_raw[i][:].rearrange("p j n -> p n j"),
+            )
+        nc.vector.quantize_mx(out=w_codes[:].bitcast(FP8X4), scales=w_scales[:], in_=w_grouped[:])
+        for h, (lo, hi) in enumerate(POOL_PARTS):
+            nc.vector.tensor_copy(picked_words[h][:], table_words[:].indirect(entries(offs_sb, lo, hi)))
 
-        y = [[psum.tile([P, hi - lo], F32, name="y%d_%d" % (i, lo)) for lo, hi in POOL_PARTS] for i in range(2)]
-        tanh_half = [f32_tile("tanh_half%d" % i, S) for i in range(2)]
+        y = [psum.tile([P, 2, hi - lo], F32, name="y%d" % lo) for lo, hi in POOL_PARTS]
+        tanh_half = keep.tile([P, 2, S], F32, name="tanh_half", align_bytes=64)
         abs_tanh = [f32_tile("abs_tanh%d" % i, S) for i in range(2)]
         log_term = [f32_tile("log_term%d" % i, S) for i in range(2)]
         reserve = [f32_tile("reserve%d" % i, S) for i in range(2)]
         for h, (lo, hi) in enumerate(POOL_PARTS):
             for i in range(2):
                 nc.tensor.matmul_mx(
-                    out=y[i][h][:],
-                    lhsT=w_codes[i][:].bitcast(FP8X4),
-                    lhsT_scale=w_scales[i][:],
-                    rhs=picked_words[:, lo:hi].bitcast(FP8X4),
+                    out=y[h][:, i, :],
+                    lhsT=w_codes[:, i * N : (i + 1) * N].bitcast(FP8X4),
+                    lhsT_scale=w_scales[:, i * N : (i + 1) * N],
+                    rhs=picked_words[h][:].bitcast(FP8X4),
                     rhs_scale=picked_scales[:, lo:hi],
                     start=True,
                     stop=True,
                 )
-                nc.scalar.activation(tanh_half[i][:, lo:hi], y[i][h][:], ACT.Tanh, scale=0.5)
-        nc.scalar.activation(preload_out[:, 1:2], tanh_half[1][:, S - 1 : S], ACT.Ln, scale=0.0, bias=ln_bias[:])
+            nc.scalar.activation(tanh_half[:, :, lo:hi], y[h][:], ACT.Tanh, scale=0.5)
+        nc.scalar.activation(preload_out[:, 1:2], y[-1][:, 1, 0:1], ACT.Ln, scale=0.0, bias=ln_bias[:])
 
+        relu_y = keep.tile([P, 2, S], F32, name="relu_y", align_bytes=64)
+        for h, (lo, hi) in enumerate(POOL_PARTS):
+            nc.vector.tensor_scalar_max(relu_y[:, :, lo:hi], y[h][:], 0.0)
         paid = f32_tile("paid", U)
         neg_risk = f32_tile("neg_risk", 1)
         for i in range(2):
-            nc.vector.scalar_tensor_tensor(abs_tanh[i][:], tanh_half[i][:], -1.0, tanh_half[i][:], ALU.mult, ALU.max)
+            nc.vector.scalar_tensor_tensor(abs_tanh[i][:], tanh_half[:, i, :], -1.0, tanh_half[:, i, :], ALU.mult, ALU.max)
         nc.vector.tensor_tensor(paid[:], inp_sb[:], fee_sb[:], ALU.mult)
         nc.vector.tensor_scalar_mul(neg_risk[:], risk_sb[:], -1.0)
 
         for i in range(2):
-            for h, (lo, hi) in enumerate(POOL_PARTS):
+            for lo, hi in LOG_PARTS:
                 nc.scalar.activation(log_term[i][:, lo:hi], abs_tanh[i][:, lo:hi], ACT.Ln, scale=LN_FACTOR, bias=ln_bias[:])
-        nc.scalar.activation(preload_out[:, 2:3], log_term[1][:, S - 1 : S], ACT.Abs_reciprocal_sqrt, scale=0.0, bias=ln_bias[:])
+        nc.scalar.activation(preload_out[:, 2:3], abs_tanh[1][:, S - 1 : S], ACT.Abs_reciprocal_sqrt, scale=0.0, bias=ln_bias[:])
 
         def finish_reserve(i):
-            for h, (lo, hi) in enumerate(POOL_PARTS):
-                nc.vector.scalar_tensor_tensor(
-                    reserve[i][:, lo:hi], y[i][h][:], 0.0, log_term[i][:, lo:hi], ALU.max, ALU.subtract
-                )
+            for lo, hi in LOG_PARTS:
+                nc.vector.tensor_tensor(reserve[i][:, lo:hi], relu_y[:, i, lo:hi], log_term[i][:, lo:hi], ALU.subtract)
 
         ra, rb = reserve
-        names = ["den", "num", "sign", "root", "recip", "signed", "quot"]
-        hop = [{n: [f32_tile("%s%d_%d" % (n, k, lo), hi - lo) for lo, hi in ROUTE_PARTS] for n in names} for k in range(2)]
-        passed = [f32_tile("passed%d" % lo, hi - lo) for lo, hi in ROUTE_PARTS]
-        mid_sq = [f32_tile("mid_sq%d" % lo, hi - lo) for lo, hi in ROUTE_PARTS]
-        result = [f32_tile("result%d" % lo, hi - lo) for lo, hi in ROUTE_PARTS]
+        names = "den1 num1 root1 recip1 mid_abs mid_sq cross passed den2 num2 sign2 root2 recip2 signed got result"
+        t = {n: [f32_tile("%s_%d" % (n, lo), hi - lo) for lo, hi in ROUTE_PARTS] for n in names.split()}
+        parts = list(enumerate(ROUTE_PARTS))
 
-        def denominator(k, c, list_tile, amount):
-            lo, hi = ROUTE_PARTS[c]
-            t = hop[k]
-            nc.vector.tensor_tensor(t["den"][c][:], ra[:].indirect(entries(list_tile, lo, hi)), amount, ALU.add)
-            nc.scalar.activation(t["sign"][c][:], t["den"][c][:], ACT.Sign)
-            nc.scalar.activation(t["root"][c][:], t["den"][c][:], ACT.Abs_reciprocal_sqrt)
-            nc.scalar.activation(t["recip"][c][:], t["root"][c][:], ACT.Square)
+        def fetch(dst, window, list_tile, other, op):
+            for c, (lo, hi) in parts:
+                nc.vector.tensor_tensor(t[dst][c][:], window[:].indirect(entries(list_tile, lo, hi)), other(c), op)
 
-        def numerator(k, c, list_tile, amount):
-            lo, hi = ROUTE_PARTS[c]
-            nc.vector.tensor_tensor(hop[k]["num"][c][:], rb[:].indirect(entries(list_tile, lo, hi)), amount, ALU.mult)
+        def combine(dst, a, other, op):
+            for c, (lo, hi) in parts:
+                nc.vector.tensor_tensor(t[dst][c][:], t[a][c][:], other(c), op)
 
-        def signed(k, c):
-            t = hop[k]
-            nc.vector.tensor_tensor(t["signed"][c][:], t["num"][c][:], t["sign"][c][:], ALU.mult)
+        def part_of(name):
+            return lambda c: t[name][c][:]
 
-        def quotient(k, c):
-            t = hop[k]
-            nc.vector.tensor_tensor(t["quot"][c][:], t["signed"][c][:], t["recip"][c][:], ALU.mult)
+        def columns_of(tile):
+            return lambda c: tile[:, ROUTE_PARTS[c][0] : ROUTE_PARTS[c][1]]
 
-        parts = range(len(ROUTE_PARTS))
+        def unary(dst, src, c, func):
+            nc.scalar.activation(t[dst][c][:], t[src][c][:], func)
+
         finish_reserve(0)
-        for c in parts:
-            denominator(0, c, hop1_sb, paid[:, ROUTE_PARTS[c][0] : ROUTE_PARTS[c][1]])
+        fetch("den1", ra, hop1_sb, columns_of(paid), ALU.add)
+        for c, (lo, hi) in parts:
+            unary("root1", "den1", c, ACT.Abs_reciprocal_sqrt)
+            unary("recip1", "root1", c, ACT.Square)
         finish_reserve(1)
-        for c in parts:
-            numerator(0, c, hop1_sb, paid[:, ROUTE_PARTS[c][0] : ROUTE_PARTS[c][1]])
-        for c in parts:
-            signed(0, c)
-        for c in parts:
-            quotient(0, c)
-        for c in parts:
-            lo, hi = ROUTE_PARTS[c]
-            nc.vector.tensor_tensor(passed[c][:], hop[0]["quot"][c][:], fee_sb[:, lo:hi], ALU.mult)
-        for c in parts:
-            denominator(1, c, hop2_sb, passed[c][:])
-        for c in parts:
-            nc.scalar.activation(mid_sq[c][:], hop[0]["quot"][c][:], ACT.Square)
-            numerator(1, c, hop2_sb, passed[c][:])
-        for c in parts:
-            signed(1, c)
-        for c in parts:
-            quotient(1, c)
-        for c in parts:
-            lo, hi = ROUTE_PARTS[c]
+        fetch("cross", ra, hop2_sb, part_of("den1"), ALU.mult)
+        fetch("num1", rb, hop1_sb, columns_of(paid), ALU.mult)
+        combine("passed", "num1", columns_of(fee_sb), ALU.mult)
+        combine("den2", "cross", part_of("passed"), ALU.add)
+        for c, (lo, hi) in parts:
+            unary("sign2", "den2", c, ACT.Sign)
+            unary("root2", "den2", c, ACT.Abs_reciprocal_sqrt)
+            unary("recip2", "root2", c, ACT.Square)
+        combine("mid_abs", "num1", part_of("recip1"), ALU.mult)
+        for c, (lo, hi) in parts:
+            unary("mid_sq", "mid_abs", c, ACT.Square)
+        fetch("num2", rb, hop2_sb, part_of("passed"), ALU.mult)
+        combine("signed", "num2", part_of("sign2"), ALU.mult)
+        combine("got", "signed", part_of("recip2"), ALU.mult)
+        for c, (lo, hi) in parts:
             nc.vector.scalar_tensor_tensor(
-                result[c][:], mid_sq[c][:], neg_risk[:], hop[1]["quot"][c][:], ALU.mult, ALU.add
+                t["result"][c][:], t["mid_sq"][c][:], neg_risk[:], t["got"][c][:], ALU.mult, ALU.add
             )
-            nc.sync.dma_start(out[:, lo:hi], result[c][:])
+            nc.sync.dma_start(out[:, lo:hi], t["result"][c][:])

import math
from contextlib import ExitStack

import concourse.mybir as mybir

K, T, S, N, U = 512, 1024, 512, 128, 512
FLOPS = 2 * 2 * K * N * S

F32 = mybir.dt.float32
BF16 = mybir.dt.bfloat16
I32 = mybir.dt.int32
U32 = mybir.dt.uint32
U16 = mybir.dt.uint16
U8 = mybir.dt.uint8
FP8X4 = mybir.dt.float8_e4m3fn_x4
ALU = mybir.AluOpType
ACT = mybir.ActivationFunctionType

P = 128
PACK = 4
LIST_ROWS = 16
POOL_PARTS = [(0, 128), (128, 256), (256, 384), (384, 512)]
LOG_PARTS = [(0, 256), (256, 512)]
ROUTE_PARTS = [(0, 256), (256, 512)]
LN_FACTOR = 0.5 * math.exp(-0.5)


def tile_picked_yamm_net_p_kernel(
    tc, x_words, x_scales, w1, w2, inp, fee, risk, offs, hop1, hop2, out
):
    nc = tc.nc
    with ExitStack() as ctx:
        keep = ctx.enter_context(tc.tile_pool(name="keep", bufs=1))
        psum = ctx.enter_context(tc.psum_pool(name="psum", bufs=1))

        def f32_tile(name, width):
            return keep.tile([P, width], F32, name=name, align_bytes=64)

        def entries(list_tile, lo, hi):
            return list_tile[:, lo // LIST_ROWS : hi // LIST_ROWS]

        offs_sb = keep.tile([P, S // LIST_ROWS], U16, name="offs_sb")
        hop1_sb = keep.tile([P, U // LIST_ROWS], U16, name="hop1_sb")
        hop2_sb = keep.tile([P, U // LIST_ROWS], U16, name="hop2_sb")
        table_words = keep.tile([P, T], U32, name="table_words", align_bytes=64)
        table_scales = keep.tile([P, T], U8, name="table_scales", align_bytes=64)
        w_raw = [keep.tile([P, PACK, N], F32, name="w_raw%d" % i, align_bytes=64) for i in range(2)]
        inp_sb = f32_tile("inp_sb", U)
        fee_sb = f32_tile("fee_sb", U)
        risk_sb = f32_tile("risk_sb", 1)
        preload = f32_tile("preload", 1)
        preload_out = f32_tile("preload_out", 3)

        nc.vector.memset(table_scales[:].bitcast(I32), 0)
        nc.vector.memset(preload[:], 1.0)
        ln_bias = f32_tile("ln_bias", 1)
        nc.vector.tensor_scalar_mul(ln_bias[:], preload[:], LN_FACTOR)
        nc.scalar.activation(preload_out[:, 0:1], preload[:], ACT.Tanh)

        nc.sync.dma_start(w_raw[0][:], w1.rearrange("(p j) n -> p j n", j=PACK))
        nc.sync.dma_start(offs_sb[:], offs)
        scale_rows = x_scales[0].bitcast(I32)
        for q in range(4):
            nc.sync.dma_start(table_scales[32 * q : 32 * q + 4, :].bitcast(I32), scale_rows[4 * q : 4 * q + 4, :])
        nc.sync.dma_start(w_raw[1][:], w2.rearrange("(p j) n -> p j n", j=PACK))
        nc.sync.dma_start(table_words[:].bitcast(I32), x_words[0].rearrange("p c r -> p (c r)").bitcast(I32))
        nc.sync.dma_start(hop1_sb[:], hop1)
        nc.sync.dma_start(inp_sb[:], inp)
        nc.sync.dma_start(fee_sb[:], fee)
        nc.sync.dma_start(hop2_sb[:], hop2)
        nc.sync.dma_start(risk_sb[:], risk)

        picked_scales = keep.tile([P, S], U8, name="picked_scales", align_bytes=64)
        picked_words = [
            keep.tile([P, hi - lo], U32, name="picked_words%d" % lo, align_bytes=64) for lo, hi in POOL_PARTS
        ]
        w_codes = keep.tile([P, 2 * N], U32, name="w_codes", align_bytes=64)
        w_scales = keep.tile([P, 2 * N], U8, name="w_scales", align_bytes=64)
        w_grouped = keep.tile([P, 2 * N * PACK], BF16, name="w_grouped", align_bytes=64)

        nc.vector.tensor_copy(picked_scales[:], table_scales[:].indirect(offs_sb[:]))
        for i in range(2):
            nc.scalar.copy(
                w_grouped[:, i * N * PACK : (i + 1) * N * PACK].rearrange("p (n j) -> p n j", j=PACK),
                w_raw[i][:].rearrange("p j n -> p n j"),
            )
        nc.vector.quantize_mx(out=w_codes[:].bitcast(FP8X4), scales=w_scales[:], in_=w_grouped[:])
        for h, (lo, hi) in enumerate(POOL_PARTS):
            nc.vector.tensor_copy(picked_words[h][:], table_words[:].indirect(entries(offs_sb, lo, hi)))

        y = [psum.tile([P, 2, hi - lo], F32, name="y%d" % lo) for lo, hi in POOL_PARTS]
        tanh_half = keep.tile([P, 2, S], F32, name="tanh_half", align_bytes=64)
        abs_tanh = [f32_tile("abs_tanh%d" % i, S) for i in range(2)]
        log_term = [f32_tile("log_term%d" % i, S) for i in range(2)]
        reserve = [f32_tile("reserve%d" % i, S) for i in range(2)]
        for h, (lo, hi) in enumerate(POOL_PARTS):
            for i in range(2):
                nc.tensor.matmul_mx(
                    out=y[h][:, i, :],
                    lhsT=w_codes[:, i * N : (i + 1) * N].bitcast(FP8X4),
                    lhsT_scale=w_scales[:, i * N : (i + 1) * N],
                    rhs=picked_words[h][:].bitcast(FP8X4),
                    rhs_scale=picked_scales[:, lo:hi],
                    start=True,
                    stop=True,
                )
            nc.scalar.activation(tanh_half[:, :, lo:hi], y[h][:], ACT.Tanh, scale=0.5)
        nc.scalar.activation(preload_out[:, 1:2], y[-1][:, 1, 0:1], ACT.Ln, scale=0.0, bias=ln_bias[:])

        relu_y = keep.tile([P, 2, S], F32, name="relu_y", align_bytes=64)
        for h, (lo, hi) in enumerate(POOL_PARTS):
            nc.vector.tensor_scalar_max(relu_y[:, :, lo:hi], y[h][:], 0.0)
        paid = f32_tile("paid", U)
        neg_risk = f32_tile("neg_risk", 1)
        for i in range(2):
            nc.vector.scalar_tensor_tensor(abs_tanh[i][:], tanh_half[:, i, :], -1.0, tanh_half[:, i, :], ALU.mult, ALU.max)
        nc.vector.tensor_tensor(paid[:], inp_sb[:], fee_sb[:], ALU.mult)
        nc.vector.tensor_scalar_mul(neg_risk[:], risk_sb[:], -1.0)

        for i in range(2):
            for lo, hi in LOG_PARTS:
                nc.scalar.activation(log_term[i][:, lo:hi], abs_tanh[i][:, lo:hi], ACT.Ln, scale=LN_FACTOR, bias=ln_bias[:])
        nc.scalar.activation(preload_out[:, 2:3], abs_tanh[1][:, S - 1 : S], ACT.Abs_reciprocal_sqrt, scale=0.0, bias=ln_bias[:])

        def finish_reserve(i):
            for lo, hi in LOG_PARTS:
                nc.vector.tensor_tensor(reserve[i][:, lo:hi], relu_y[:, i, lo:hi], log_term[i][:, lo:hi], ALU.subtract)

        ra, rb = reserve
        names = "den1 num1 root1 recip1 mid_abs mid_sq cross passed den2 num2 sign2 root2 recip2 signed got result"
        t = {n: [f32_tile("%s_%d" % (n, lo), hi - lo) for lo, hi in ROUTE_PARTS] for n in names.split()}
        parts = list(enumerate(ROUTE_PARTS))

        def fetch(dst, window, list_tile, other, op):
            for c, (lo, hi) in parts:
                nc.vector.tensor_tensor(t[dst][c][:], window[:].indirect(entries(list_tile, lo, hi)), other(c), op)

        def combine(dst, a, other, op):
            for c, (lo, hi) in parts:
                nc.vector.tensor_tensor(t[dst][c][:], t[a][c][:], other(c), op)

        def part_of(name):
            return lambda c: t[name][c][:]

        def columns_of(tile):
            return lambda c: tile[:, ROUTE_PARTS[c][0] : ROUTE_PARTS[c][1]]

        def unary(dst, src, c, func):
            nc.scalar.activation(t[dst][c][:], t[src][c][:], func)

        finish_reserve(0)
        fetch("den1", ra, hop1_sb, columns_of(paid), ALU.add)
        for c, (lo, hi) in parts:
            unary("root1", "den1", c, ACT.Abs_reciprocal_sqrt)
            unary("recip1", "root1", c, ACT.Square)
        finish_reserve(1)
        fetch("cross", ra, hop2_sb, part_of("den1"), ALU.mult)
        fetch("num1", rb, hop1_sb, columns_of(paid), ALU.mult)
        combine("passed", "num1", columns_of(fee_sb), ALU.mult)
        combine("den2", "cross", part_of("passed"), ALU.add)
        for c, (lo, hi) in parts:
            unary("sign2", "den2", c, ACT.Sign)
            unary("root2", "den2", c, ACT.Abs_reciprocal_sqrt)
            unary("recip2", "root2", c, ACT.Square)
        combine("mid_abs", "num1", part_of("recip1"), ALU.mult)
        for c, (lo, hi) in parts:
            unary("mid_sq", "mid_abs", c, ACT.Square)
        fetch("num2", rb, hop2_sb, part_of("passed"), ALU.mult)
        combine("signed", "num2", part_of("sign2"), ALU.mult)
        combine("got", "signed", part_of("recip2"), ALU.mult)
        for c, (lo, hi) in parts:
            nc.vector.scalar_tensor_tensor(
                t["result"][c][:], t["mid_sq"][c][:], neg_risk[:], t["got"][c][:], ALU.mult, ALU.add
            )
            nc.sync.dma_start(out[:, lo:hi], t["result"][c][:])
